import numpy as np
import ml_dtypes


def mxq(x, axis, fmt="e4m3"):
    dtype, down = {"e4m3": (ml_dtypes.float8_e4m3fn, 7), "e5m2": (ml_dtypes.float8_e5m2, 14)}[fmt]
    v = np.moveaxis(np.asarray(x, np.float32).astype(ml_dtypes.bfloat16).astype(np.float64), axis, -1)
    blocks = v.reshape(v.shape[:-1] + (-1, 32))
    amax = np.abs(blocks).max(-1, keepdims=True)
    byte = np.maximum(np.where(amax > 0, np.frexp(amax)[1] - 1 + 127, 0) - down, 1)
    scale = np.exp2(byte - 127.0)
    codes = (blocks / scale).astype(np.float32).astype(dtype).astype(np.float64)
    return np.moveaxis((codes * scale).reshape(v.shape), -1, axis)


WIDE = False


def mx_kscale(k):
    if not WIDE:
        return np.ones(k)
    levels = np.array([10, -10, 5, -5, 0])
    if k % 512:
        return np.exp2(np.random.permutation(np.resize(levels, k // 32))).repeat(32)
    a = np.empty((k // 512, 16))
    for p in range(k // 512):
        a[p, :8] = np.random.permutation(np.resize(levels, 8))
        for g in range(8):
            far = levels[np.abs(levels - a[p, g]) >= 10]
            a[p, g + 8] = far[np.random.randint(len(far))]
    return np.exp2(a.ravel()).repeat(32)


def f64(x):
    return np.asarray(x).astype(np.float64)


def striped(idx):
    return np.tile(idx.reshape(-1, 16).T, (8, 1)).astype(np.uint16)


def unstriped(offs):
    return offs[:16].T.reshape(-1).astype(np.int64)


def striped8(idx):
    return np.concatenate([x.reshape(-1, 16).T for x in idx]).astype(np.uint16)


def runs(offs, k):
    lists = np.stack([offs[16 * r : 16 * r + 16].T.reshape(-1) for r in range(8)]).astype(np.int64)
    return lists[np.arange(k) % 512 // 64]


def pack_weight(w):
    k, n = w.shape
    w = f64(np.asarray(w, np.float32).astype(ml_dtypes.bfloat16)).reshape(k // 32, 32, n)
    amax = np.abs(w).max(1)
    byte = np.clip(np.where(amax > 0, np.frexp(amax)[1] - 1 + 127 - 7, 1), 1, 254)
    scaled = (w * np.exp2(127.0 - byte)[:, None, :]).reshape(k, n).astype(np.float32)
    words = np.ascontiguousarray(scaled.reshape(k // 512, 128, 4, n).transpose(0, 1, 3, 2)).astype(ml_dtypes.float8_e4m3fn).view(np.uint8)
    return words, np.ascontiguousarray(byte.astype(np.uint8).reshape(k // 512, 16, n))


def unpack_weight(words, scales):
    g, p, n, _ = words.shape
    vals = np.ascontiguousarray(words).view(ml_dtypes.float8_e4m3fn).astype(np.float64) * np.repeat(np.exp2(scales.astype(np.float64) - 127.0), 8, axis=1)[..., None]
    return vals.transpose(0, 1, 3, 2).reshape(g * 512, n)


def relu(v):
    return np.maximum(v, 0.0)

def planes(y):
    n, m = y.shape
    v = y.astype(np.float32).astype(ml_dtypes.bfloat16).astype(np.float64).reshape(n // 32, 32, m)
    top = np.abs(v).max(1)
    byte = np.clip(np.where(top > 0, np.frexp(top)[1] - 1 + 127 - 7, 1), 1, 254)
    codes = (v * np.exp2(127.0 - byte)[:, None, :]).reshape(n, m).astype(np.float32).astype(ml_dtypes.float8_e4m3fn).view(np.uint8)
    words = codes.reshape(n // 512, 128, 4, m).transpose(0, 1, 3, 2)
    return np.ascontiguousarray(words), np.ascontiguousarray(byte.astype(np.uint8).reshape(n // 512, 16, m))


K, T, S, V, N, H = 512, 2048, 512, 256, 512, 512


def setup_inputs():
    n = np.random.standard_normal
    s = mx_kscale(K)[:, None]
    u = mx_kscale(H)
    packed_xT = pack_weight(n((K, T)) * s)
    packed_w3 = pack_weight(n((H, N)) / np.sqrt(H) / u[:, None])
    return {
        "x_words": packed_xT[0],
        "x_scales": packed_xT[1],
        "w1": (n((K, H)) / np.sqrt(K) / s * u).astype(np.float32),
        "w2": (n((H, H)) / np.sqrt(H) / u[:, None] * u).astype(np.float32),
        "w3_words": packed_w3[0],
        "w3_scales": packed_w3[1],
        "res": n((N, S)).astype(np.float32),
        "offs": striped(np.random.permutation(T)[:S]),
        "order": striped8(np.stack([np.random.permutation(S) for _ in range(8)])),
        "at": striped8(np.stack([np.random.permutation(S)[:V] for _ in range(8)])),
    }


def reference(x_words, x_scales, w1, w2, w3_words, w3_scales, res, offs, order, at):
    xq = unpack_weight(x_words, x_scales)[:, unstriped(offs)]
    y = mxq(f64(w1), 0, "e4m3").T @ xq
    o = y[np.arange(H)[:, None], runs(order, H)]
    z = o.reshape(H, V, 2).max(axis=2)
    h = relu(mxq(f64(w2), 0, "e4m3").T @ mxq(z, 0, "e4m3"))
    z2 = y.copy()
    z2[np.arange(H)[:, None], runs(at, H)] = h
    out_0 = f64(res) + (unpack_weight(w3_words, w3_scales).T @ mxq(z2, 0, "e4m3"))
    return (out_0,) + planes(out_0)

@@ -1,0 +1,215 @@
+from contextlib import ExitStack
+
+import concourse.mybir as mybir
+
+K, T, S, V, N, H = 512, 2048, 512, 256, 512, 512
+FLOPS = 2 * K * H * S + 2 * H * H * V + 2 * H * N * S
+
+F32 = mybir.dt.float32
+BF16 = mybir.dt.bfloat16
+I32 = mybir.dt.int32
+U32 = mybir.dt.uint32
+U16 = mybir.dt.uint16
+U8 = mybir.dt.uint8
+FP8X4 = mybir.dt.float8_e4m3fn_x4
+ALU = mybir.AluOpType
+ACT = mybir.ActivationFunctionType
+
+P = 128
+PACK = 4
+HALF = S // 2
+VH = V // 2
+CHUNK = 128
+LIST = 16
+
+
+def tile_picked_poolback_none_po_kernel(
+    tc, x_words, x_scales, w1, w2, w3_words, w3_scales, res, offs, order, at, out_0, out_1, out_2
+):
+    nc = tc.nc
+    with ExitStack() as ctx:
+        keep = ctx.enter_context(tc.tile_pool(name="keep", bufs=1))
+        psum = ctx.enter_context(tc.psum_pool(name="psum", bufs=8))
+
+        def tile(name, shape, dtype, tag=None):
+            return keep.tile(shape, dtype, name=name, tag=tag or name, align_bytes=64)
+
+        def bank(name):
+            return psum.tile([P, 512], F32, name=name, tag="bank")
+
+        def as_words(packed):
+            return packed[0].rearrange("p c r -> p (c r)").bitcast(I32)
+
+        def load_scale_rows(queue, plane, rows):
+            for q in range(4):
+                queue.dma_start(out=plane[32 * q : 32 * q + 4, :].bitcast(I32), in_=rows[0].bitcast(I32)[4 * q : 4 * q + 4, :])
+
+        def load_weight(name, w, c0, c1):
+            raw = tile(name, [P, PACK, c1 - c0], F32)
+            nc.sync.dma_start(out=raw[:], in_=w.rearrange("(p j) c -> p j c", j=PACK)[:, :, c0:c1])
+            return raw
+
+        def deal_views(grouped, raw, first, m0, m1):
+            dst = grouped[:].rearrange("p (t m j) -> p m j t", t=PACK, j=PACK)[:, m0:m1]
+            src = raw[:].rearrange("p j (m t) -> p m j t", t=PACK)[:, m0 - first : m1 - first]
+            return dst, src
+
+        def quantize(codes, scales, values):
+            nc.vector.quantize_mx(out=codes.bitcast(FP8X4), scales=scales, in_=values)
+
+        def product(out, w_codes, w_scales, t, codes, scales):
+            cols = slice(P * t, P * (t + 1))
+            nc.tensor.matmul_mx(out=out, lhsT=w_codes[:, cols].bitcast(FP8X4), lhsT_scale=w_scales[:, cols],
+                                rhs=codes.bitcast(FP8X4), rhs_scale=scales, start=True, stop=True)
+
+        offs_t = keep.tile([P, S // LIST], U16, name="offs_t")
+        order_t = keep.tile([P, S // LIST], U16, name="order_t")
+        at_t = keep.tile([P, V // LIST], U16, name="at_t")
+        xw = tile("xw", [P, T], I32)
+        xs = tile("xs", [P, T], U8)
+        w3s = tile("w3s", [P, N], U8)
+        w3w = tile("w3w", [P, N], I32)
+        res_t = tile("res_t", [P, PACK, S], F32)
+
+        nc.vector.memset(xs[:].bitcast(I32), 0)
+        nc.vector.memset(w3s[:].bitcast(I32), 0)
+
+        nc.sync.dma_start(offs_t[:], offs)
+        w1a = load_weight("w1a", w1, 0, HALF)
+        nc.sync.dma_start(order_t[:], order)
+        load_scale_rows(nc.sync, xs, x_scales)
+        w1b = load_weight("w1b", w1, HALF, H)
+        nc.sync.dma_start(out=xw[:], in_=as_words(x_words))
+        nc.sync.dma_start(out=w3w[:], in_=as_words(w3_words))
+        load_scale_rows(nc.sync, w3s, w3_scales)
+        w2_raw = load_weight("w2_raw", w2, 0, H)
+        nc.sync.dma_start(at_t[:], at)
+        nc.sync.dma_start(out=res_t[:], in_=res.rearrange("(p t) j -> p t j", t=PACK))
+
+        xqs = tile("xqs", [P, S], U8)
+        nc.vector.tensor_copy(xqs[:], xs[:].indirect(offs_t[:]))
+
+        w1g = tile("w1g", [P, PACK * H], BF16)
+        d, s = deal_views(w1g, w1a, 0, 0, 64)
+        nc.scalar.activation(d, s, ACT.Copy)
+        d, s = deal_views(w1g, w1b, 64, 64, 88)
+        nc.scalar.copy(d, s)
+        d, s = deal_views(w1g, w1b, 64, 88, 128)
+        nc.vector.tensor_copy(d, s)
+        w1c = tile("w1c", [P, H], I32)
+        w1s = tile("w1s", [P, H], U8)
+        quantize(w1c[:], w1s[:], w1g[:])
+
+        xqw = tile("xqw", [P, S], I32)
+        for h in range(2):
+            cols = slice(h * HALF, (h + 1) * HALF)
+            nc.vector.tensor_copy(xqw[:, cols].bitcast(U32), xw[:].bitcast(U32).indirect(offs_t[:, 16 * h : 16 * h + 16]))
+
+        w3c = tile("w3c", [P, N], I32)
+        w3d = tile("w3d", [P, N], U8)
+        nc.vector.tensor_copy(w3d[:].rearrange("p (t m) -> p m t", t=PACK), w3s[:].rearrange("p (m t) -> p m t", t=PACK))
+        nc.vector.tensor_copy(w3c[:].rearrange("p (t m) -> p m t", t=PACK), w3w[:].rearrange("p (m t) -> p m t", t=PACK))
+
+        y = [tile("y%d" % t, [P, S], F32) for t in range(PACK)]
+        for t in range(PACK):
+            for h in range(2):
+                cols = slice(h * HALF, (h + 1) * HALF)
+                acc = bank("yacc")
+                product(acc[:, :HALF], w1c, w1s, t, xqw[:, cols], xqs[:, cols])
+                nc.scalar.copy(y[t][:, cols], acc[:, :HALF])
+
+        w2g = tile("w2g", [P, PACK * H], BF16)
+        d, s = deal_views(w2g, w2_raw, 0, 0, 128)
+        nc.scalar.copy(d, s)
+        w2c = tile("w2c", [P, H], I32)
+        w2s = tile("w2s", [P, H], U8)
+
+        slots = tile("slots", [P, (PACK + 1) * HALF], F32)
+        g = [slots[:, HALF:].rearrange("p (t j) -> p t j", t=PACK), slots[:, : PACK * HALF].rearrange("p (t j) -> p t j", t=PACK)]
+        zg = [tile("zg0", [P, VH * PACK], BF16)]
+        zc = [tile("zc%d" % h, [P, VH], I32) for h in range(2)]
+        zs = [tile("zs%d" % h, [P, VH], U8) for h in range(2)]
+        hid = tile("hid", [P, PACK, V], F32)
+
+        def gather(t, h):
+            nc.vector.tensor_copy(g[h][:, t, :], y[t][:].indirect(order_t[:, 16 * h : 16 * h + 16]))
+
+        def pool_pairs(h):
+            pairs = g[h].rearrange("p t (a b e) -> p a t b e", b=2, e=2)
+            nc.vector.tensor_tensor(zg[h][:].rearrange("p (a b t) -> p a t b", b=2, t=PACK), pairs[:, :, :, :, 0], pairs[:, :, :, :, 1], ALU.max)
+
+        def hidden(h):
+            for t in range(PACK):
+                acc = bank("hacc")
+                product(acc[:, :VH], w2c, w2s, t, zc[h][:], zs[h][:])
+                nc.scalar.activation(hid[:, t, VH * h : VH * (h + 1)], acc[:, :VH], ACT.Relu)
+
+        def scatter(t, h0, h1):
+            nc.vector.tensor_copy(y[t][:].indirect(at_t[:, 8 * h0 : 8 * h1]), hid[:, t, VH * h0 : VH * h1])
+
+        z2g = tile("z2g", [P, S * PACK], BF16)
+
+        def round_plane(copy, t, c0, c1):
+            copy(z2g[:].rearrange("p (j t) -> p j t", t=PACK)[:, c0:c1, t], y[t][:, c0:c1])
+
+        gather(0, 0)
+        gather(0, 1)
+        gather(1, 0)
+        gather(2, 0)
+        gather(3, 0)
+        pool_pairs(0)
+        gather(1, 1)
+        quantize(zc[0][:], zs[0][:], zg[0][:])
+        gather(2, 1)
+        gather(3, 1)
+        quantize(w2c[:], w2s[:], w2g[:])
+        hidden(0)
+        zg.append(tile("zg1", [P, VH * PACK], BF16, tag="w2g"))
+        pool_pairs(1)
+        scatter(0, 0, 1)
+        quantize(zc[1][:], zs[1][:], zg[1][:])
+        hidden(1)
+        scatter(1, 0, 1)
+        scatter(0, 1, 2)
+        round_plane(nc.scalar.copy, 0, 0, S)
+        scatter(1, 1, 2)
+        round_plane(nc.scalar.copy, 1, 0, S)
+        scatter(2, 0, 2)
+        round_plane(nc.scalar.copy, 2, CHUNK, S)
+        scatter(3, 0, 2)
+        round_plane(nc.vector.tensor_copy, 2, 0, CHUNK)
+
+        z2c = tile("z2c", [P, S], I32)
+        z2s = tile("z2s", [P, S], U8)
+        o = tile("o", [P, PACK, S], F32)
+        og = tile("og", [P, S * PACK], BF16)
+        oc = tile("oc", [P, S], I32)
+        osc = tile("osc", [P, S], U8)
+        out_rows = out_0.rearrange("(p t) j -> p t j", t=PACK)
+        out_words = as_words(out_1)
+        chunks = S // CHUNK
+
+        def cols(c):
+            return slice(CHUNK * c, CHUNK * (c + 1))
+
+        def wide(c):
+            return slice(PACK * CHUNK * c, PACK * CHUNK * (c + 1))
+
+        accs = []
+        for c in range(chunks):
+            round_plane(nc.vector.tensor_copy if c == 0 else nc.scalar.copy, 3, CHUNK * c, CHUNK * (c + 1))
+            quantize(z2c[:, cols(c)], z2s[:, cols(c)], z2g[:, wide(c)])
+            acc = bank("oacc")
+            for t in range(PACK):
+                product(acc[:, CHUNK * t : CHUNK * (t + 1)], w3c, w3d, t, z2c[:, cols(c)], z2s[:, cols(c)])
+            accs.append(acc)
+        for c in range(chunks):
+            nc.vector.tensor_tensor(o[:, :, cols(c)], accs[c][:].rearrange("p (t j) -> p t j", t=PACK), res_t[:, :, cols(c)], ALU.add)
+            nc.sync.dma_start(out=out_rows[:, :, cols(c)], in_=o[:, :, cols(c)])
+            nc.scalar.copy(og[:, wide(c)].rearrange("p (a i t) -> p a t i", i=4, t=PACK), o[:, :, cols(c)].rearrange("p t (a i) -> p a t i", i=4))
+        for c in range(chunks):
+            quantize(oc[:, cols(c)], osc[:, cols(c)], og[:, wide(c)])
+            nc.sync.dma_start(out=out_words[:, cols(c)], in_=oc[:, cols(c)])
+        for q in range(4):
+            queue = nc.sync if q % 2 == 0 else nc.scalar
+            queue.dma_start(out=out_2[0].bitcast(I32)[4 * q : 4 * q + 4, :], in_=osc[32 * q : 32 * q + 4, :].bitcast(I32))

@@ -74,12 +74,12 @@ def tile_picked_poolback_none_po_kernel(
         nc.vector.memset(xs[:].bitcast(I32), 0)
         nc.vector.memset(w3s[:].bitcast(I32), 0)
 
-        nc.sync.dma_start(offs_t[:], offs)
         w1a = load_weight("w1a", w1, 0, HALF)
-        nc.sync.dma_start(order_t[:], order)
+        nc.sync.dma_start(offs_t[:], offs)
         load_scale_rows(nc.sync, xs, x_scales)
         w1b = load_weight("w1b", w1, HALF, H)
         nc.sync.dma_start(out=xw[:], in_=as_words(x_words))
+        nc.sync.dma_start(order_t[:], order)
         nc.sync.dma_start(out=w3w[:], in_=as_words(w3_words))
         load_scale_rows(nc.sync, w3s, w3_scales)
         w2_raw = load_weight("w2_raw", w2, 0, H)
@@ -126,17 +126,20 @@ def tile_picked_poolback_none_po_kernel(
 
         slots = tile("slots", [P, (PACK + 1) * HALF], F32)
         g = [slots[:, HALF:].rearrange("p (t j) -> p t j", t=PACK), slots[:, : PACK * HALF].rearrange("p (t j) -> p t j", t=PACK)]
-        zg = [tile("zg0", [P, VH * PACK], BF16)]
+        zg = [tile("zg0", [P, VH * PACK], BF16)[:], w2g[:, : VH * PACK]]
         zc = [tile("zc%d" % h, [P, VH], I32) for h in range(2)]
         zs = [tile("zs%d" % h, [P, VH], U8) for h in range(2)]
         hid = tile("hid", [P, PACK, V], F32)
+
+        def quantize_w2(t0, t1):
+            quantize(w2c[:, P * t0 : P * t1], w2s[:, P * t0 : P * t1], w2g[:, PACK * P * t0 : PACK * P * t1])
 
         def gather(t, h):
             nc.vector.tensor_copy(g[h][:, t, :], y[t][:].indirect(order_t[:, 16 * h : 16 * h + 16]))
 
         def pool_pairs(h):
             pairs = g[h].rearrange("p t (a b e) -> p a t b e", b=2, e=2)
-            nc.vector.tensor_tensor(zg[h][:].rearrange("p (a b t) -> p a t b", b=2, t=PACK), pairs[:, :, :, :, 0], pairs[:, :, :, :, 1], ALU.max)
+            nc.vector.tensor_tensor(zg[h].rearrange("p (a b t) -> p a t b", b=2, t=PACK), pairs[:, :, :, :, 0], pairs[:, :, :, :, 1], ALU.max)
 
         def hidden(h):
             for t in range(PACK):
@@ -159,25 +162,25 @@ def tile_picked_poolback_none_po_kernel(
         gather(3, 0)
         pool_pairs(0)
         gather(1, 1)
-        quantize(zc[0][:], zs[0][:], zg[0][:])
+        quantize(zc[0][:], zs[0][:], zg[0])
         gather(2, 1)
         gather(3, 1)
-        quantize(w2c[:], w2s[:], w2g[:])
-        hidden(0)
-        zg.append(tile("zg1", [P, VH * PACK], BF16, tag="w2g"))
+        quantize_w2(0, 1)
+        quantize_w2(1, 2)
         pool_pairs(1)
-        scatter(0, 0, 1)
-        quantize(zc[1][:], zs[1][:], zg[1][:])
+        quantize_w2(2, 4)
+        quantize(zc[1][:], zs[1][:], zg[1])
+        hidden(0)
         hidden(1)
+        scatter(0, 0, 1)
         scatter(1, 0, 1)
         scatter(0, 1, 2)
         round_plane(nc.scalar.copy, 0, 0, S)
         scatter(1, 1, 2)
         round_plane(nc.scalar.copy, 1, 0, S)
         scatter(2, 0, 2)
-        round_plane(nc.scalar.copy, 2, CHUNK, S)
+        round_plane(nc.scalar.copy, 2, 2 * CHUNK, S)
         scatter(3, 0, 2)
-        round_plane(nc.vector.tensor_copy, 2, 0, CHUNK)
 
         z2c = tile("z2c", [P, S], I32)
         z2s = tile("z2s", [P, S], U8)
@@ -197,7 +200,9 @@ def tile_picked_poolback_none_po_kernel(
 
         accs = []
         for c in range(chunks):
-            round_plane(nc.vector.tensor_copy if c == 0 else nc.scalar.copy, 3, CHUNK * c, CHUNK * (c + 1))
+            if c < 2:
+                round_plane(nc.vector.tensor_copy, 2, CHUNK * c, CHUNK * (c + 1))
+            round_plane(nc.vector.tensor_copy if c < 2 else nc.scalar.copy, 3, CHUNK * c, CHUNK * (c + 1))
             quantize(z2c[:, cols(c)], z2s[:, cols(c)], z2g[:, wide(c)])
             acc = bank("oacc")
             for t in range(PACK):

@@ -41,8 +41,8 @@ def tile_picked_poolback_none_po_kernel(
             return packed[0].rearrange("p c r -> p (c r)").bitcast(I32)
 
         def load_scale_rows(queue, plane, rows):
-            for q in range(4):
-                queue.dma_start(out=plane[32 * q : 32 * q + 4, :].bitcast(I32), in_=rows[0].bitcast(I32)[4 * q : 4 * q + 4, :])
+            for r in range(4):
+                queue.dma_start(out=plane[r:P:32, :].bitcast(I32), in_=rows[0].bitcast(I32)[r:16:4, :])
 
         def load_weight(name, w, c0, c1):
             raw = tile(name, [P, PACK, c1 - c0], F32)
@@ -120,7 +120,8 @@ def tile_picked_poolback_none_po_kernel(
 
         w2g = tile("w2g", [P, PACK * H], BF16)
         d, s = deal_views(w2g, w2_raw, 0, 0, 128)
-        nc.scalar.copy(d, s)
+        nc.scalar.copy(d[:, :, :, 0:2], s[:, :, :, 0:2])
+        nc.scalar.copy(d[:, :, :, 2:4], s[:, :, :, 2:4])
         w2c = tile("w2c", [P, H], I32)
         w2s = tile("w2s", [P, H], U8)
 
@@ -179,7 +180,7 @@ def tile_picked_poolback_none_po_kernel(
         scatter(1, 1, 2)
         round_plane(nc.scalar.copy, 1, 0, S)
         scatter(2, 0, 2)
-        round_plane(nc.scalar.copy, 2, 2 * CHUNK, S)
+        round_plane(nc.scalar.copy, 2, HALF, S)
         scatter(3, 0, 2)
 
         z2c = tile("z2c", [P, S], I32)
@@ -209,12 +210,20 @@ def tile_picked_poolback_none_po_kernel(
                 product(acc[:, CHUNK * t : CHUNK * (t + 1)], w3c, w3d, t, z2c[:, cols(c)], z2s[:, cols(c)])
             accs.append(acc)
         for c in range(chunks):
-            nc.vector.tensor_tensor(o[:, :, cols(c)], accs[c][:].rearrange("p (t j) -> p t j", t=PACK), res_t[:, :, cols(c)], ALU.add)
+            pieces = 1
+            width = CHUNK // pieces
+            for i in range(pieces):
+                c0 = CHUNK * c + width * i
+                sums = accs[c][:].rearrange("p (t j) -> p t j", t=PACK)[:, :, width * i : width * (i + 1)]
+                nc.vector.tensor_tensor(o[:, :, c0 : c0 + width], sums, res_t[:, :, c0 : c0 + width], ALU.add)
+                nc.scalar.copy(
+                    og[:, PACK * c0 : PACK * (c0 + width)].rearrange("p (a i t) -> p a t i", i=4, t=PACK),
+                    o[:, :, c0 : c0 + width].rearrange("p t (a i) -> p a t i", i=4),
+                )
             nc.sync.dma_start(out=out_rows[:, :, cols(c)], in_=o[:, :, cols(c)])
-            nc.scalar.copy(og[:, wide(c)].rearrange("p (a i t) -> p a t i", i=4, t=PACK), o[:, :, cols(c)].rearrange("p t (a i) -> p a t i", i=4))
         for c in range(chunks):
             quantize(oc[:, cols(c)], osc[:, cols(c)], og[:, wide(c)])
             nc.sync.dma_start(out=out_words[:, cols(c)], in_=oc[:, cols(c)])
-        for q in range(4):
-            queue = nc.sync if q % 2 == 0 else nc.scalar
-            queue.dma_start(out=out_2[0].bitcast(I32)[4 * q : 4 * q + 4, :], in_=osc[32 * q : 32 * q + 4, :].bitcast(I32))
+        for r in range(4):
+            queue = nc.sync if r % 2 == 0 else nc.scalar
+            queue.dma_start(out=out_2[0].bitcast(I32)[r:16:4, :], in_=osc[r:P:32, :].bitcast(I32))

@@ -16,11 +16,17 @@ ALU = mybir.AluOpType
 ACT = mybir.ActivationFunctionType
 
 P = 128
-PACK = 4
+PLANES = 4
+QUADRANT = 32
+SCALE_ROWS = 16
+LIST_ROWS = 16
+BANK = 512
 HALF = S // 2
-VH = V // 2
+POOLED = V // 2
 CHUNK = 128
-LIST = 16
+CHUNKS = S // CHUNK
+W1_SCALAR_END = 88
+VECTOR_CHUNKS = 2
 
 
 def tile_picked_poolback_none_po_kernel(
@@ -31,199 +37,252 @@ def tile_picked_poolback_none_po_kernel(
         keep = ctx.enter_context(tc.tile_pool(name="keep", bufs=1))
         psum = ctx.enter_context(tc.psum_pool(name="psum", bufs=8))
 
-        def tile(name, shape, dtype, tag=None):
-            return keep.tile(shape, dtype, name=name, tag=tag or name, align_bytes=64)
+        def tile(name, shape, dtype):
+            return keep.tile(shape, dtype, name=name, align_bytes=64)
 
         def bank(name):
-            return psum.tile([P, 512], F32, name=name, tag="bank")
+            return psum.tile([P, BANK], F32, name=name, tag="bank")
 
         def as_words(packed):
             return packed[0].rearrange("p c r -> p (c r)").bitcast(I32)
 
-        def load_scale_rows(queue, plane, rows):
+        def scale_rows(plane, rows, r):
+            return plane[r:P:QUADRANT, :].bitcast(I32), rows[0].bitcast(I32)[r:SCALE_ROWS:4, :]
+
+        def load_scale_rows(plane, rows):
             for r in range(4):
-                queue.dma_start(out=plane[r:P:32, :].bitcast(I32), in_=rows[0].bitcast(I32)[r:16:4, :])
+                on_chip, in_hbm = scale_rows(plane, rows, r)
+                nc.sync.dma_start(out=on_chip, in_=in_hbm)
 
         def load_weight(name, w, c0, c1):
-            raw = tile(name, [P, PACK, c1 - c0], F32)
-            nc.sync.dma_start(out=raw[:], in_=w.rearrange("(p j) c -> p j c", j=PACK)[:, :, c0:c1])
+            raw = tile(name, [P, PLANES, c1 - c0], F32)
+            nc.sync.dma_start(out=raw[:], in_=w.rearrange("(p j) c -> p j c", j=PLANES)[:, :, c0:c1])
             return raw
 
         def deal_views(grouped, raw, first, m0, m1):
-            dst = grouped[:].rearrange("p (t m j) -> p m j t", t=PACK, j=PACK)[:, m0:m1]
-            src = raw[:].rearrange("p j (m t) -> p m j t", t=PACK)[:, m0 - first : m1 - first]
+            dst = grouped[:].rearrange("p (t m j) -> p m j t", t=PLANES, j=PLANES)[:, m0:m1]
+            src = raw[:].rearrange("p j (m t) -> p m j t", t=PLANES)[:, m0 - first : m1 - first]
             return dst, src
 
         def quantize(codes, scales, values):
             nc.vector.quantize_mx(out=codes.bitcast(FP8X4), scales=scales, in_=values)
 
         def product(out, w_codes, w_scales, t, codes, scales):
-            cols = slice(P * t, P * (t + 1))
-            nc.tensor.matmul_mx(out=out, lhsT=w_codes[:, cols].bitcast(FP8X4), lhsT_scale=w_scales[:, cols],
-                                rhs=codes.bitcast(FP8X4), rhs_scale=scales, start=True, stop=True)
+            plane = slice(P * t, P * (t + 1))
+            nc.tensor.matmul_mx(
+                out=out,
+                lhsT=w_codes[:, plane].bitcast(FP8X4),
+                lhsT_scale=w_scales[:, plane],
+                rhs=codes.bitcast(FP8X4),
+                rhs_scale=scales,
+                start=True,
+                stop=True,
+            )
 
-        offs_t = keep.tile([P, S // LIST], U16, name="offs_t")
-        order_t = keep.tile([P, S // LIST], U16, name="order_t")
-        at_t = keep.tile([P, V // LIST], U16, name="at_t")
-        xw = tile("xw", [P, T], I32)
-        xs = tile("xs", [P, T], U8)
-        w3s = tile("w3s", [P, N], U8)
-        w3w = tile("w3w", [P, N], I32)
-        res_t = tile("res_t", [P, PACK, S], F32)
+        def entries(list_tile, first, last):
+            return list_tile[:, first // LIST_ROWS : last // LIST_ROWS]
 
-        nc.vector.memset(xs[:].bitcast(I32), 0)
-        nc.vector.memset(w3s[:].bitcast(I32), 0)
+        offs_list = keep.tile([P, S // LIST_ROWS], U16, name="offs_list")
+        order_list = keep.tile([P, S // LIST_ROWS], U16, name="order_list")
+        at_list = keep.tile([P, V // LIST_ROWS], U16, name="at_list")
+        x_word_table = tile("x_word_table", [P, T], I32)
+        x_scale_table = tile("x_scale_table", [P, T], U8)
+        w3_scales_raw = tile("w3_scales_raw", [P, N], U8)
+        w3_words_raw = tile("w3_words_raw", [P, N], I32)
+        residual = tile("residual", [P, PLANES, S], F32)
 
-        w1a = load_weight("w1a", w1, 0, HALF)
-        nc.sync.dma_start(offs_t[:], offs)
-        load_scale_rows(nc.sync, xs, x_scales)
-        w1b = load_weight("w1b", w1, HALF, H)
-        nc.sync.dma_start(out=xw[:], in_=as_words(x_words))
-        nc.sync.dma_start(order_t[:], order)
-        nc.sync.dma_start(out=w3w[:], in_=as_words(w3_words))
-        load_scale_rows(nc.sync, w3s, w3_scales)
+        nc.vector.memset(x_scale_table[:].bitcast(I32), 0)
+        nc.vector.memset(w3_scales_raw[:].bitcast(I32), 0)
+
+        w1_left = load_weight("w1_left", w1, 0, H // 2)
+        nc.sync.dma_start(offs_list[:], offs)
+        load_scale_rows(x_scale_table, x_scales)
+        w1_right = load_weight("w1_right", w1, H // 2, H)
+        nc.sync.dma_start(out=x_word_table[:], in_=as_words(x_words))
+        nc.sync.dma_start(order_list[:], order)
+        nc.sync.dma_start(out=w3_words_raw[:], in_=as_words(w3_words))
+        load_scale_rows(w3_scales_raw, w3_scales)
         w2_raw = load_weight("w2_raw", w2, 0, H)
-        nc.sync.dma_start(at_t[:], at)
-        nc.sync.dma_start(out=res_t[:], in_=res.rearrange("(p t) j -> p t j", t=PACK))
+        nc.sync.dma_start(at_list[:], at)
+        nc.sync.dma_start(out=residual[:], in_=res.rearrange("(p t) j -> p t j", t=PLANES))
 
-        xqs = tile("xqs", [P, S], U8)
-        nc.vector.tensor_copy(xqs[:], xs[:].indirect(offs_t[:]))
+        x_scale = tile("x_scale", [P, S], U8)
+        nc.vector.tensor_copy(x_scale[:], x_scale_table[:].indirect(offs_list[:]))
 
-        w1g = tile("w1g", [P, PACK * H], BF16)
-        d, s = deal_views(w1g, w1a, 0, 0, 64)
-        nc.scalar.activation(d, s, ACT.Copy)
-        d, s = deal_views(w1g, w1b, 64, 64, 88)
-        nc.scalar.copy(d, s)
-        d, s = deal_views(w1g, w1b, 64, 88, 128)
-        nc.vector.tensor_copy(d, s)
-        w1c = tile("w1c", [P, H], I32)
-        w1s = tile("w1s", [P, H], U8)
-        quantize(w1c[:], w1s[:], w1g[:])
+        w1_grouped = tile("w1_grouped", [P, PLANES * H], BF16)
+        nc.scalar.activation(*deal_views(w1_grouped, w1_left, 0, 0, P // 2), ACT.Copy)
+        nc.scalar.copy(*deal_views(w1_grouped, w1_right, P // 2, P // 2, W1_SCALAR_END))
+        nc.vector.tensor_copy(*deal_views(w1_grouped, w1_right, P // 2, W1_SCALAR_END, P))
+        w1_code = tile("w1_code", [P, H], I32)
+        w1_scale = tile("w1_scale", [P, H], U8)
+        quantize(w1_code[:], w1_scale[:], w1_grouped[:])
 
-        xqw = tile("xqw", [P, S], I32)
-        for h in range(2):
-            cols = slice(h * HALF, (h + 1) * HALF)
-            nc.vector.tensor_copy(xqw[:, cols].bitcast(U32), xw[:].bitcast(U32).indirect(offs_t[:, 16 * h : 16 * h + 16]))
+        x_code = tile("x_code", [P, S], I32)
+        for first in (0, HALF):
+            window = x_word_table[:].bitcast(U32).indirect(entries(offs_list, first, first + HALF))
+            nc.vector.tensor_copy(x_code[:, first : first + HALF].bitcast(U32), window)
 
-        w3c = tile("w3c", [P, N], I32)
-        w3d = tile("w3d", [P, N], U8)
-        nc.vector.tensor_copy(w3d[:].rearrange("p (t m) -> p m t", t=PACK), w3s[:].rearrange("p (m t) -> p m t", t=PACK))
-        nc.vector.tensor_copy(w3c[:].rearrange("p (t m) -> p m t", t=PACK), w3w[:].rearrange("p (m t) -> p m t", t=PACK))
+        w3_code = tile("w3_code", [P, N], I32)
+        w3_scale = tile("w3_scale", [P, N], U8)
+        for dealt, raw in ((w3_scale, w3_scales_raw), (w3_code, w3_words_raw)):
+            nc.vector.tensor_copy(
+                dealt[:].rearrange("p (t m) -> p m t", t=PLANES), raw[:].rearrange("p (m t) -> p m t", t=PLANES)
+            )
 
-        y = [tile("y%d" % t, [P, S], F32) for t in range(PACK)]
-        for t in range(PACK):
-            for h in range(2):
-                cols = slice(h * HALF, (h + 1) * HALF)
-                acc = bank("yacc")
-                product(acc[:, :HALF], w1c, w1s, t, xqw[:, cols], xqs[:, cols])
-                nc.scalar.copy(y[t][:, cols], acc[:, :HALF])
+        y = [tile("y%d" % t, [P, S], F32) for t in range(PLANES)]
 
-        w2g = tile("w2g", [P, PACK * H], BF16)
-        d, s = deal_views(w2g, w2_raw, 0, 0, 128)
-        nc.scalar.copy(d[:, :, :, 0:2], s[:, :, :, 0:2])
-        nc.scalar.copy(d[:, :, :, 2:4], s[:, :, :, 2:4])
-        w2c = tile("w2c", [P, H], I32)
-        w2s = tile("w2s", [P, H], U8)
+        def project(t, first, last, copy):
+            acc = bank("y_sums")
+            product(acc[:, : last - first], w1_code, w1_scale, t, x_code[:, first:last], x_scale[:, first:last])
+            copy(y[t][:, first:last], acc[:, : last - first])
 
-        slots = tile("slots", [P, (PACK + 1) * HALF], F32)
-        g = [slots[:, HALF:].rearrange("p (t j) -> p t j", t=PACK), slots[:, : PACK * HALF].rearrange("p (t j) -> p t j", t=PACK)]
-        zg = [tile("zg0", [P, VH * PACK], BF16)[:], w2g[:, : VH * PACK]]
-        zc = [tile("zc%d" % h, [P, VH], I32) for h in range(2)]
-        zs = [tile("zs%d" % h, [P, VH], U8) for h in range(2)]
-        hid = tile("hid", [P, PACK, V], F32)
+        project(0, 0, HALF, nc.scalar.copy)
+        project(0, HALF, HALF + P, nc.scalar.copy)
+        project(0, HALF + P, S, nc.vector.tensor_copy)
+        for t in range(1, PLANES):
+            project(t, 0, HALF, nc.scalar.copy)
+            project(t, HALF, S, nc.scalar.copy)
+
+        w2_grouped = tile("w2_grouped", [P, PLANES * H], BF16)
+        dst, src = deal_views(w2_grouped, w2_raw, 0, 0, P)
+        nc.scalar.copy(dst[:, :, :, 0:2], src[:, :, :, 0:2])
+        nc.scalar.copy(dst[:, :, :, 2:4], src[:, :, :, 2:4])
+        w2_code = tile("w2_code", [P, H], I32)
+        w2_scale = tile("w2_scale", [P, H], U8)
+
+        slots = tile("slots", [P, 2 * PLANES * HALF], F32)
+        lined_up = [
+            slots[:, HALF : (PLANES + 1) * HALF].rearrange("p (t j) -> p t j", t=PLANES),
+            slots[:].rearrange("p (t u j) -> p t u j", t=PLANES, u=2)[:, :, 0, :],
+        ]
+        z_grouped = [tile("z_first", [P, POOLED * PLANES], BF16)[:], w2_grouped[:, : POOLED * PLANES]]
+        z_code = [tile("z_code%d" % h, [P, POOLED], I32) for h in range(2)]
+        z_scale = [tile("z_scale%d" % h, [P, POOLED], U8) for h in range(2)]
+        hidden = tile("hidden", [P, PLANES, V], F32)
 
         def quantize_w2(t0, t1):
-            quantize(w2c[:, P * t0 : P * t1], w2s[:, P * t0 : P * t1], w2g[:, PACK * P * t0 : PACK * P * t1])
+            quantize(
+                w2_code[:, P * t0 : P * t1],
+                w2_scale[:, P * t0 : P * t1],
+                w2_grouped[:, PLANES * P * t0 : PLANES * P * t1],
+            )
 
         def gather(t, h):
-            nc.vector.tensor_copy(g[h][:, t, :], y[t][:].indirect(order_t[:, 16 * h : 16 * h + 16]))
+            window = y[t][:].indirect(entries(order_list, HALF * h, HALF * (h + 1)))
+            nc.vector.tensor_copy(lined_up[h][:, t, :], window)
 
         def pool_pairs(h):
-            pairs = g[h].rearrange("p t (a b e) -> p a t b e", b=2, e=2)
-            nc.vector.tensor_tensor(zg[h].rearrange("p (a b t) -> p a t b", b=2, t=PACK), pairs[:, :, :, :, 0], pairs[:, :, :, :, 1], ALU.max)
+            pairs = lined_up[h].rearrange("p t (a b e) -> p a t b e", b=2, e=2)
+            pooled = z_grouped[h].rearrange("p (a b t) -> p a t b", b=2, t=PLANES)
+            nc.vector.tensor_tensor(pooled, pairs[:, :, :, :, 0], pairs[:, :, :, :, 1], ALU.max)
 
-        def hidden(h):
-            for t in range(PACK):
-                acc = bank("hacc")
-                product(acc[:, :VH], w2c, w2s, t, zc[h][:], zs[h][:])
-                nc.scalar.activation(hid[:, t, VH * h : VH * (h + 1)], acc[:, :VH], ACT.Relu)
+        def quantize_z(h):
+            quantize(z_code[h][:], z_scale[h][:], z_grouped[h])
 
-        def scatter(t, h0, h1):
-            nc.vector.tensor_copy(y[t][:].indirect(at_t[:, 8 * h0 : 8 * h1]), hid[:, t, VH * h0 : VH * h1])
+        def hidden_half(h):
+            for t in range(PLANES):
+                acc = bank("h_sums")
+                product(acc[:, :POOLED], w2_code, w2_scale, t, z_code[h][:], z_scale[h][:])
+                nc.scalar.activation(hidden[:, t, POOLED * h : POOLED * (h + 1)], acc[:, :POOLED], ACT.Relu)
 
-        z2g = tile("z2g", [P, S * PACK], BF16)
+        def scatter(t, first, last):
+            nc.vector.tensor_copy(y[t][:].indirect(entries(at_list, first, last)), hidden[:, t, first:last])
 
-        def round_plane(copy, t, c0, c1):
-            copy(z2g[:].rearrange("p (j t) -> p j t", t=PACK)[:, c0:c1, t], y[t][:, c0:c1])
+        z2_grouped = tile("z2_grouped", [P, S * PLANES], BF16)
+
+        def round_z2(copy, t, first, last):
+            dst = z2_grouped[:].rearrange("p (j t) -> p j t", t=PLANES)[:, first:last, t]
+            copy(dst, y[t][:, first:last])
 
         gather(0, 0)
         gather(0, 1)
-        gather(1, 0)
-        gather(2, 0)
-        gather(3, 0)
+        for t in range(1, PLANES):
+            gather(t, 0)
+        gather(3, 1)
         pool_pairs(0)
         gather(1, 1)
-        quantize(zc[0][:], zs[0][:], zg[0])
+        quantize_z(0)
         gather(2, 1)
-        gather(3, 1)
         quantize_w2(0, 1)
         quantize_w2(1, 2)
         pool_pairs(1)
         quantize_w2(2, 4)
-        quantize(zc[1][:], zs[1][:], zg[1])
-        hidden(0)
-        hidden(1)
-        scatter(0, 0, 1)
-        scatter(1, 0, 1)
-        scatter(0, 1, 2)
-        round_plane(nc.scalar.copy, 0, 0, S)
-        scatter(1, 1, 2)
-        round_plane(nc.scalar.copy, 1, 0, S)
-        scatter(2, 0, 2)
-        round_plane(nc.scalar.copy, 2, HALF, S)
-        scatter(3, 0, 2)
+        quantize_z(1)
+        hidden_half(0)
+        hidden_half(1)
 
-        z2c = tile("z2c", [P, S], I32)
-        z2s = tile("z2s", [P, S], U8)
-        o = tile("o", [P, PACK, S], F32)
-        og = tile("og", [P, S * PACK], BF16)
-        oc = tile("oc", [P, S], I32)
-        osc = tile("osc", [P, S], U8)
-        out_rows = out_0.rearrange("(p t) j -> p t j", t=PACK)
+        scatter(0, 0, POOLED)
+        scatter(1, 0, POOLED)
+        for t in (0, 1):
+            scatter(t, POOLED, V)
+            round_z2(nc.scalar.copy, t, 0, S)
+        scatter(2, 0, V)
+        round_z2(nc.scalar.copy, 2, VECTOR_CHUNKS * CHUNK, S)
+        scatter(3, 0, V)
+
+        z2_code = tile("z2_code", [P, S], I32)
+        z2_scale = tile("z2_scale", [P, S], U8)
+        result = tile("result", [P, PLANES, S], F32)
+        result_grouped = tile("result_grouped", [P, S * PLANES], BF16)
+        result_code = tile("result_code", [P, S], I32)
+        result_scale = tile("result_scale", [P, S], U8)
+        out_rows = out_0.rearrange("(p t) j -> p t j", t=PLANES)
         out_words = as_words(out_1)
-        chunks = S // CHUNK
 
-        def cols(c):
-            return slice(CHUNK * c, CHUNK * (c + 1))
-
-        def wide(c):
-            return slice(PACK * CHUNK * c, PACK * CHUNK * (c + 1))
-
-        accs = []
-        for c in range(chunks):
-            if c < 2:
-                round_plane(nc.vector.tensor_copy, 2, CHUNK * c, CHUNK * (c + 1))
-            round_plane(nc.vector.tensor_copy if c < 2 else nc.scalar.copy, 3, CHUNK * c, CHUNK * (c + 1))
-            quantize(z2c[:, cols(c)], z2s[:, cols(c)], z2g[:, wide(c)])
-            acc = bank("oacc")
-            for t in range(PACK):
-                product(acc[:, CHUNK * t : CHUNK * (t + 1)], w3c, w3d, t, z2c[:, cols(c)], z2s[:, cols(c)])
-            accs.append(acc)
-        for c in range(chunks):
-            pieces = 1
-            width = CHUNK // pieces
-            for i in range(pieces):
-                c0 = CHUNK * c + width * i
-                sums = accs[c][:].rearrange("p (t j) -> p t j", t=PACK)[:, :, width * i : width * (i + 1)]
-                nc.vector.tensor_tensor(o[:, :, c0 : c0 + width], sums, res_t[:, :, c0 : c0 + width], ALU.add)
-                nc.scalar.copy(
-                    og[:, PACK * c0 : PACK * (c0 + width)].rearrange("p (a i t) -> p a t i", i=4, t=PACK),
-                    o[:, :, c0 : c0 + width].rearrange("p t (a i) -> p a t i", i=4),
+        sums = []
+        for first in range(0, S, CHUNK):
+            last = first + CHUNK
+            if first < VECTOR_CHUNKS * CHUNK:
+                round_z2(nc.vector.tensor_copy, 2, first, last)
+                round_z2(nc.vector.tensor_copy, 3, first, last)
+            else:
+                round_z2(nc.scalar.copy, 3, first, last)
+            quantize(z2_code[:, first:last], z2_scale[:, first:last], z2_grouped[:, PLANES * first : PLANES * last])
+            acc = bank("out_sums")
+            for t in range(PLANES):
+                product(
+                    acc[:, CHUNK * t : CHUNK * (t + 1)],
+                    w3_code,
+                    w3_scale,
+                    t,
+                    z2_code[:, first:last],
+                    z2_scale[:, first:last],
                 )
-            nc.sync.dma_start(out=out_rows[:, :, cols(c)], in_=o[:, :, cols(c)])
-        for c in range(chunks):
-            quantize(oc[:, cols(c)], osc[:, cols(c)], og[:, wide(c)])
-            nc.sync.dma_start(out=out_words[:, cols(c)], in_=oc[:, cols(c)])
-        for r in range(4):
-            queue = nc.sync if r % 2 == 0 else nc.scalar
-            queue.dma_start(out=out_2[0].bitcast(I32)[r:16:4, :], in_=osc[r:P:32, :].bitcast(I32))
+            sums.append(acc)
+
+        def round_result(copy, first, last):
+            copy(
+                result_grouped[:, PLANES * first : PLANES * last].rearrange("p (a i t) -> p a t i", i=4, t=PLANES),
+                result[:, :, first:last].rearrange("p t (a i) -> p a t i", i=4),
+            )
+
+        for c, acc in enumerate(sums):
+            first, last = CHUNK * c, CHUNK * (c + 1)
+            nc.vector.tensor_tensor(
+                result[:, :, first:last],
+                acc[:].rearrange("p (t j) -> p t j", t=PLANES),
+                residual[:, :, first:last],
+                ALU.add,
+            )
+            nc.sync.dma_start(out=out_rows[:, :, first:last], in_=result[:, :, first:last])
+            if c < CHUNKS - 1:
+                round_result(nc.scalar.copy, first, last)
+            else:
+                round_result(nc.scalar.copy, first, last - CHUNK // 2)
+                round_result(nc.vector.tensor_copy, last - CHUNK // 2, last)
+
+        def quantize_result(first, last):
+            quantize(
+                result_code[:, first:last],
+                result_scale[:, first:last],
+                result_grouped[:, PLANES * first : PLANES * last],
+            )
+
+        quantize_result(0, HALF)
+        nc.sync.dma_start(out=out_words[:, :HALF], in_=result_code[:, :HALF])
+        quantize_result(HALF, S - CHUNK)
+        quantize_result(S - CHUNK, S)
+        nc.sync.dma_start(out=out_words[:, HALF:], in_=result_code[:, HALF:])
+        for r, queue in enumerate((nc.sync, nc.scalar, nc.sync, nc.scalar)):
+            on_chip, in_hbm = scale_rows(result_scale, out_2, r)
+            queue.dma_start(out=in_hbm, in_=on_chip)

from contextlib import ExitStack

import concourse.mybir as mybir

K, T, S, V, N, H = 512, 2048, 512, 256, 512, 512
FLOPS = 2 * K * H * S + 2 * H * H * V + 2 * H * N * S

F32 = mybir.dt.float32
BF16 = mybir.dt.bfloat16
I32 = mybir.dt.int32
U32 = mybir.dt.uint32
U16 = mybir.dt.uint16
U8 = mybir.dt.uint8
FP8X4 = mybir.dt.float8_e4m3fn_x4
ALU = mybir.AluOpType
ACT = mybir.ActivationFunctionType

P = 128
PLANES = 4
QUADRANT = 32
SCALE_ROWS = 16
LIST_ROWS = 16
BANK = 512
HALF = S // 2
POOLED = V // 2
CHUNK = 128
CHUNKS = S // CHUNK
W1_SCALAR_END = 88
VECTOR_CHUNKS = 2


def tile_picked_poolback_none_po_kernel(
    tc, x_words, x_scales, w1, w2, w3_words, w3_scales, res, offs, order, at, out_0, out_1, out_2
):
    nc = tc.nc
    with ExitStack() as ctx:
        keep = ctx.enter_context(tc.tile_pool(name="keep", bufs=1))
        psum = ctx.enter_context(tc.psum_pool(name="psum", bufs=8))

        def tile(name, shape, dtype):
            return keep.tile(shape, dtype, name=name, align_bytes=64)

        def bank(name):
            return psum.tile([P, BANK], F32, name=name, tag="bank")

        def as_words(packed):
            return packed[0].rearrange("p c r -> p (c r)").bitcast(I32)

        def scale_rows(plane, rows, r):
            return plane[r:P:QUADRANT, :].bitcast(I32), rows[0].bitcast(I32)[r:SCALE_ROWS:4, :]

        def load_scale_rows(plane, rows):
            for r in range(4):
                on_chip, in_hbm = scale_rows(plane, rows, r)
                nc.sync.dma_start(out=on_chip, in_=in_hbm)

        def load_weight(name, w, c0, c1):
            raw = tile(name, [P, PLANES, c1 - c0], F32)
            nc.sync.dma_start(out=raw[:], in_=w.rearrange("(p j) c -> p j c", j=PLANES)[:, :, c0:c1])
            return raw

        def deal_views(grouped, raw, first, m0, m1):
            dst = grouped[:].rearrange("p (t m j) -> p m j t", t=PLANES, j=PLANES)[:, m0:m1]
            src = raw[:].rearrange("p j (m t) -> p m j t", t=PLANES)[:, m0 - first : m1 - first]
            return dst, src

        def quantize(codes, scales, values):
            nc.vector.quantize_mx(out=codes.bitcast(FP8X4), scales=scales, in_=values)

        def product(out, w_codes, w_scales, t, codes, scales):
            plane = slice(P * t, P * (t + 1))
            nc.tensor.matmul_mx(
                out=out,
                lhsT=w_codes[:, plane].bitcast(FP8X4),
                lhsT_scale=w_scales[:, plane],
                rhs=codes.bitcast(FP8X4),
                rhs_scale=scales,
                start=True,
                stop=True,
            )

        def entries(list_tile, first, last):
            return list_tile[:, first // LIST_ROWS : last // LIST_ROWS]

        offs_list = keep.tile([P, S // LIST_ROWS], U16, name="offs_list")
        order_list = keep.tile([P, S // LIST_ROWS], U16, name="order_list")
        at_list = keep.tile([P, V // LIST_ROWS], U16, name="at_list")
        x_word_table = tile("x_word_table", [P, T], I32)
        x_scale_table = tile("x_scale_table", [P, T], U8)
        w3_scales_raw = tile("w3_scales_raw", [P, N], U8)
        w3_words_raw = tile("w3_words_raw", [P, N], I32)
        residual = tile("residual", [P, PLANES, S], F32)

        nc.vector.memset(x_scale_table[:].bitcast(I32), 0)
        nc.vector.memset(w3_scales_raw[:].bitcast(I32), 0)

        w1_left = load_weight("w1_left", w1, 0, H // 2)
        nc.sync.dma_start(offs_list[:], offs)
        load_scale_rows(x_scale_table, x_scales)
        w1_right = load_weight("w1_right", w1, H // 2, H)
        nc.sync.dma_start(out=x_word_table[:], in_=as_words(x_words))
        nc.sync.dma_start(order_list[:], order)
        nc.sync.dma_start(out=w3_words_raw[:], in_=as_words(w3_words))
        load_scale_rows(w3_scales_raw, w3_scales)
        w2_raw = load_weight("w2_raw", w2, 0, H)
        nc.sync.dma_start(at_list[:], at)
        nc.sync.dma_start(out=residual[:], in_=res.rearrange("(p t) j -> p t j", t=PLANES))

        x_scale = tile("x_scale", [P, S], U8)
        nc.vector.tensor_copy(x_scale[:], x_scale_table[:].indirect(offs_list[:]))

        w1_grouped = tile("w1_grouped", [P, PLANES * H], BF16)
        nc.scalar.activation(*deal_views(w1_grouped, w1_left, 0, 0, P // 2), ACT.Copy)
        nc.scalar.copy(*deal_views(w1_grouped, w1_right, P // 2, P // 2, W1_SCALAR_END))
        nc.vector.tensor_copy(*deal_views(w1_grouped, w1_right, P // 2, W1_SCALAR_END, P))
        w1_code = tile("w1_code", [P, H], I32)
        w1_scale = tile("w1_scale", [P, H], U8)
        quantize(w1_code[:], w1_scale[:], w1_grouped[:])

        x_code = tile("x_code", [P, S], I32)
        for first in (0, HALF):
            window = x_word_table[:].bitcast(U32).indirect(entries(offs_list, first, first + HALF))
            nc.vector.tensor_copy(x_code[:, first : first + HALF].bitcast(U32), window)

        w3_code = tile("w3_code", [P, N], I32)
        w3_scale = tile("w3_scale", [P, N], U8)
        for dealt, raw in ((w3_scale, w3_scales_raw), (w3_code, w3_words_raw)):
            nc.vector.tensor_copy(
                dealt[:].rearrange("p (t m) -> p m t", t=PLANES), raw[:].rearrange("p (m t) -> p m t", t=PLANES)
            )

        y = [tile("y%d" % t, [P, S], F32) for t in range(PLANES)]

        def project(t, first, last, copy):
            acc = bank("y_sums")
            product(acc[:, : last - first], w1_code, w1_scale, t, x_code[:, first:last], x_scale[:, first:last])
            copy(y[t][:, first:last], acc[:, : last - first])

        project(0, 0, HALF, nc.scalar.copy)
        project(0, HALF, HALF + P, nc.scalar.copy)
        project(0, HALF + P, S, nc.vector.tensor_copy)
        for t in range(1, PLANES):
            project(t, 0, HALF, nc.scalar.copy)
            project(t, HALF, S, nc.scalar.copy)

        w2_grouped = tile("w2_grouped", [P, PLANES * H], BF16)
        dst, src = deal_views(w2_grouped, w2_raw, 0, 0, P)
        nc.scalar.copy(dst[:, :, :, 0:2], src[:, :, :, 0:2])
        nc.scalar.copy(dst[:, :, :, 2:4], src[:, :, :, 2:4])
        w2_code = tile("w2_code", [P, H], I32)
        w2_scale = tile("w2_scale", [P, H], U8)

        slots = tile("slots", [P, 2 * PLANES * HALF], F32)
        lined_up = [
            slots[:, HALF : (PLANES + 1) * HALF].rearrange("p (t j) -> p t j", t=PLANES),
            slots[:].rearrange("p (t u j) -> p t u j", t=PLANES, u=2)[:, :, 0, :],
        ]
        z_grouped = [tile("z_first", [P, POOLED * PLANES], BF16)[:], w2_grouped[:, : POOLED * PLANES]]
        z_code = [tile("z_code%d" % h, [P, POOLED], I32) for h in range(2)]
        z_scale = [tile("z_scale%d" % h, [P, POOLED], U8) for h in range(2)]
        hidden = tile("hidden", [P, PLANES, V], F32)

        def quantize_w2(t0, t1):
            quantize(
                w2_code[:, P * t0 : P * t1],
                w2_scale[:, P * t0 : P * t1],
                w2_grouped[:, PLANES * P * t0 : PLANES * P * t1],
            )

        def gather(t, h):
            window = y[t][:].indirect(entries(order_list, HALF * h, HALF * (h + 1)))
            nc.vector.tensor_copy(lined_up[h][:, t, :], window)

        def pool_pairs(h):
            pairs = lined_up[h].rearrange("p t (a b e) -> p a t b e", b=2, e=2)
            pooled = z_grouped[h].rearrange("p (a b t) -> p a t b", b=2, t=PLANES)
            nc.vector.tensor_tensor(pooled, pairs[:, :, :, :, 0], pairs[:, :, :, :, 1], ALU.max)

        def quantize_z(h):
            quantize(z_code[h][:], z_scale[h][:], z_grouped[h])

        def hidden_half(h):
            for t in range(PLANES):
                acc = bank("h_sums")
                product(acc[:, :POOLED], w2_code, w2_scale, t, z_code[h][:], z_scale[h][:])
                nc.scalar.activation(hidden[:, t, POOLED * h : POOLED * (h + 1)], acc[:, :POOLED], ACT.Relu)

        def scatter(t, first, last):
            nc.vector.tensor_copy(y[t][:].indirect(entries(at_list, first, last)), hidden[:, t, first:last])

        z2_grouped = tile("z2_grouped", [P, S * PLANES], BF16)

        def round_z2(copy, t, first, last):
            dst = z2_grouped[:].rearrange("p (j t) -> p j t", t=PLANES)[:, first:last, t]
            copy(dst, y[t][:, first:last])

        gather(0, 0)
        gather(0, 1)
        for t in range(1, PLANES):
            gather(t, 0)
        gather(3, 1)
        pool_pairs(0)
        gather(1, 1)
        quantize_z(0)
        gather(2, 1)
        quantize_w2(0, 1)
        quantize_w2(1, 2)
        pool_pairs(1)
        quantize_w2(2, 4)
        quantize_z(1)
        hidden_half(0)
        hidden_half(1)

        scatter(0, 0, POOLED)
        scatter(1, 0, POOLED)
        for t in (0, 1):
            scatter(t, POOLED, V)
            round_z2(nc.scalar.copy, t, 0, S)
        scatter(2, 0, V)
        round_z2(nc.scalar.copy, 2, VECTOR_CHUNKS * CHUNK, S)
        scatter(3, 0, V)

        z2_code = tile("z2_code", [P, S], I32)
        z2_scale = tile("z2_scale", [P, S], U8)
        result = tile("result", [P, PLANES, S], F32)
        result_grouped = tile("result_grouped", [P, S * PLANES], BF16)
        result_code = tile("result_code", [P, S], I32)
        result_scale = tile("result_scale", [P, S], U8)
        out_rows = out_0.rearrange("(p t) j -> p t j", t=PLANES)
        out_words = as_words(out_1)

        sums = []
        for first in range(0, S, CHUNK):
            last = first + CHUNK
            if first < VECTOR_CHUNKS * CHUNK:
                round_z2(nc.vector.tensor_copy, 2, first, last)
                round_z2(nc.vector.tensor_copy, 3, first, last)
            else:
                round_z2(nc.scalar.copy, 3, first, last)
            quantize(z2_code[:, first:last], z2_scale[:, first:last], z2_grouped[:, PLANES * first : PLANES * last])
            acc = bank("out_sums")
            for t in range(PLANES):
                product(
                    acc[:, CHUNK * t : CHUNK * (t + 1)],
                    w3_code,
                    w3_scale,
                    t,
                    z2_code[:, first:last],
                    z2_scale[:, first:last],
                )
            sums.append(acc)

        def round_result(copy, first, last):
            copy(
                result_grouped[:, PLANES * first : PLANES * last].rearrange("p (a i t) -> p a t i", i=4, t=PLANES),
                result[:, :, first:last].rearrange("p t (a i) -> p a t i", i=4),
            )

        for c, acc in enumerate(sums):
            first, last = CHUNK * c, CHUNK * (c + 1)
            nc.vector.tensor_tensor(
                result[:, :, first:last],
                acc[:].rearrange("p (t j) -> p t j", t=PLANES),
                residual[:, :, first:last],
                ALU.add,
            )
            nc.sync.dma_start(out=out_rows[:, :, first:last], in_=result[:, :, first:last])
            if c < CHUNKS - 1:
                round_result(nc.scalar.copy, first, last)
            else:
                round_result(nc.scalar.copy, first, last - CHUNK // 2)
                round_result(nc.vector.tensor_copy, last - CHUNK // 2, last)

        def quantize_result(first, last):
            quantize(
                result_code[:, first:last],
                result_scale[:, first:last],
                result_grouped[:, PLANES * first : PLANES * last],
            )

        quantize_result(0, HALF)
        nc.sync.dma_start(out=out_words[:, :HALF], in_=result_code[:, :HALF])
        quantize_result(HALF, S - CHUNK)
        quantize_result(S - CHUNK, S)
        nc.sync.dma_start(out=out_words[:, HALF:], in_=result_code[:, HALF:])
        for r, queue in enumerate((nc.sync, nc.scalar, nc.sync, nc.scalar)):
            on_chip, in_hbm = scale_rows(result_scale, out_2, r)
            queue.dma_start(out=in_hbm, in_=on_chip)
